import numpy as np
import ml_dtypes


def mxq(x, axis, fmt="e4m3"):
    dtype, down = {"e4m3": (ml_dtypes.float8_e4m3fn, 7), "e5m2": (ml_dtypes.float8_e5m2, 14)}[fmt]
    v = np.moveaxis(np.asarray(x, np.float32).astype(ml_dtypes.bfloat16).astype(np.float64), axis, -1)
    blocks = v.reshape(v.shape[:-1] + (-1, 32))
    amax = np.abs(blocks).max(-1, keepdims=True)
    byte = np.maximum(np.where(amax > 0, np.frexp(amax)[1] - 1 + 127, 0) - down, 1)
    scale = np.exp2(byte - 127.0)
    codes = (blocks / scale).astype(np.float32).astype(dtype).astype(np.float64)
    return np.moveaxis((codes * scale).reshape(v.shape), -1, axis)


WIDE = False


def mx_kscale(k):
    if not WIDE:
        return np.ones(k)
    levels = np.array([10, -10, 5, -5, 0])
    if k % 512:
        return np.exp2(np.random.permutation(np.resize(levels, k // 32))).repeat(32)
    a = np.empty((k // 512, 16))
    for p in range(k // 512):
        a[p, :8] = np.random.permutation(np.resize(levels, 8))
        for g in range(8):
            far = levels[np.abs(levels - a[p, g]) >= 10]
            a[p, g + 8] = far[np.random.randint(len(far))]
    return np.exp2(a.ravel()).repeat(32)


def f64(x):
    return np.asarray(x).astype(np.float64)


def striped(idx):
    return np.tile(idx.reshape(-1, 16).T, (8, 1)).astype(np.uint16)


def unstriped(offs):
    return offs[:16].T.reshape(-1).astype(np.int64)


E2M1 = np.array([0.0, 0.5, 1.0, 1.5, 2.0, 3.0, 4.0, 6.0, -0.0, -0.5, -1.0, -1.5, -2.0, -3.0, -4.0, -6.0])


def pack_weight(w, fmt):
    k, n = w.shape
    w = f64(np.asarray(w, np.float32).astype(ml_dtypes.bfloat16)).reshape(k // 32, 32, n)
    amax = np.abs(w).max(1)
    if fmt == "e4m3":
        byte = np.frexp(amax)[1] - 1 + 127 - 7
    else:
        mant, ex = np.frexp(amax / 6.0)
        byte = np.where(mant > 0.5, ex, ex - 1) + 127
    byte = np.clip(np.where(amax > 0, byte, 1), 1, 254)
    scaled = (w * np.exp2(127.0 - byte)[:, None, :]).reshape(k, n).astype(np.float32)
    by_word = np.ascontiguousarray(scaled.reshape(k // 512, 128, 4, n).transpose(0, 1, 3, 2))
    if fmt == "e4m3":
        words = by_word.astype(ml_dtypes.float8_e4m3fn).view(np.uint8)
    else:
        c = by_word.astype(ml_dtypes.float4_e2m1fn).view(np.uint8) & 0xF
        words = (c[..., 0::2] | (c[..., 1::2] << 4)).reshape(k // 512, 128, 2 * n)
    return np.ascontiguousarray(words), np.ascontiguousarray(byte.astype(np.uint8).reshape(k // 512, 16, n))


def unpack_weight(words, scales, fmt):
    g, _, n = scales.shape
    words = np.ascontiguousarray(words).reshape(g, 128, n, -1)
    if fmt == "e4m3":
        vals = words.view(ml_dtypes.float8_e4m3fn).astype(np.float64)
    else:
        nib = np.empty((g, 128, n, 4), np.uint8)
        nib[..., 0::2] = words & 0xF
        nib[..., 1::2] = words >> 4
        vals = E2M1[nib]
    vals = vals * np.repeat(np.exp2(scales.astype(np.float64) - 127.0), 8, axis=1)[..., None]
    return vals.transpose(0, 1, 3, 2).reshape(g * 512, n)


def gelu(v):
    return 0.5 * v * (1.0 + np.tanh(np.sqrt(2.0 / np.pi) * (v + 0.044715 * v**3)))


def striped8(idx):
    return np.concatenate([v.reshape(-1, 16).T for v in idx]).astype(np.uint16)


def unstriped8(offs):
    return np.stack([offs[16 * g:16 * g + 16].T.reshape(-1) for g in range(8)]).astype(np.int64)


def runs(v, idx8):
    k = np.arange(v.shape[0])
    return v[k[:, None], idx8[k % 512 // 64]]


def bf(x):
    return np.asarray(x, np.float32).astype(ml_dtypes.bfloat16)


def planes(Y):
    n, m = Y.shape
    b = f64(bf(Y)).reshape(n // 32, 32, m)
    amax = np.abs(b).max(1)
    byte = np.clip(np.where(amax > 0, np.frexp(amax)[1] - 1 + 127 - 7, 1), 1, 254)
    codes = (b * np.exp2(127.0 - byte)[:, None, :]).reshape(n, m).astype(np.float32).astype(ml_dtypes.float8_e4m3fn).view(np.uint8)
    words = codes.reshape(n // 512, 128, 4, m).transpose(0, 1, 3, 2)
    return np.ascontiguousarray(words), np.ascontiguousarray(byte.astype(np.uint8).reshape(n // 512, 16, m))


K, H, N, T, S, P, L, R = 1536, 1024, 512, 2048, 1024, 512, 8, 64

def setup_inputs():
    n = np.random.standard_normal
    s = mx_kscale(K)[:, None]
    u = mx_kscale(H)[:, None]
    tab_words, tab_scales = pack_weight(n((K, T)) * s, "e4m3")
    spread = np.exp(0.8 * n(N))[None, :]
    w2_words, w2_scales = pack_weight(n((H, N)) / np.sqrt(H) / u * spread, "e2m1")
    idx8 = np.stack([np.random.permutation(S)[:P] for run in range(L)])
    return {
        "tab_words": tab_words, "tab_scales": tab_scales,
        "offs": striped(np.random.permutation(T)[:S]),
        "offs2": striped8(idx8),
        "w1": (0.8 * n((K, H)) / np.sqrt(K) / s).astype(np.float32),
        "level": (0.4 * n(H)).astype(np.float32),
        "steep": np.repeat(np.random.uniform(1, 3, H // R), R).astype(np.float32),
        "share": np.repeat(np.random.uniform(0.1, 0.5, H // R), R).astype(np.float32),
        "pattern": (1.6 * n((H, P)) * u).astype(np.float32),
        "gain": (np.random.uniform(0.5, 1.2, H) * u[:, 0]).astype(np.float32),
        "w2_words": w2_words, "w2_scales": w2_scales,
        "w3": (n((H, N)) / np.sqrt(H) / u * spread).astype(np.float32),
    }

def reference(tab_words, tab_scales, offs, offs2, w1, level, steep, share, pattern, gain, w2_words, w2_scales, w3):
    v = unpack_weight(tab_words, tab_scales, "e4m3")[:, unstriped(offs)]
    h = (mxq(f64(w1), 0, "e4m3").T @ v) + f64(level)[:, None]
    top = h.max(axis=1)
    hp = runs(h, unstriped8(offs2))
    a = 1.0 / (1.0 + np.exp(-f64(steep)[:, None] * (hp - f64(share)[:, None] * top[:, None])))
    x = mxq(a * f64(pattern), 0, "e4m3")
    z = mxq(hp * f64(gain)[:, None], 0, "e4m3")
    w2 = unpack_weight(w2_words, w2_scales, "e2m1")
    y = w2.T @ x + mxq(f64(w3), 0, "e4m3").T @ z
    words, scales = planes(y)
    return y, words, scales

@@ -1,0 +1,323 @@
+from contextlib import ExitStack
+
+import concourse.mybir as mybir
+
+K, H, N, T, S, M = 1536, 1024, 512, 2048, 1024, 512
+FLOPS = 2 * K * H * S + 2 * 2 * H * N * M
+
+F32 = mybir.dt.float32
+BF16 = mybir.dt.bfloat16
+I32 = mybir.dt.int32
+U32 = mybir.dt.uint32
+U16 = mybir.dt.uint16
+U8 = mybir.dt.uint8
+FP8X4 = mybir.dt.float8_e4m3fn_x4
+FP4X4 = mybir.dt.float4_e2m1fn_x4
+ALU = mybir.AluOpType
+ACT = mybir.ActivationFunctionType
+
+P = 128
+PACK = 4
+PASS = P * PACK
+K_PASSES = K // PASS
+H_PASSES = H // PASS
+BANK = 512
+HALF = M // 2
+LIST_ROWS = 16
+
+
+def tile_list_flank_contact_features_kernel(
+    tc, tab_words, tab_scales, offs, offs2, w1, level, steep, share, pattern, gain,
+    w2_words, w2_scales, w3, out_0, out_1, out_2,
+):
+    nc = tc.nc
+    with ExitStack() as ctx:
+        keep = ctx.enter_context(tc.tile_pool(name="keep", bufs=1))
+        raws = ctx.enter_context(tc.tile_pool(name="raws", bufs=5))
+        woven = ctx.enter_context(tc.tile_pool(name="woven", bufs=3))
+        hpool = ctx.enter_context(tc.tile_pool(name="hpool", bufs=6))
+        psum = ctx.enter_context(tc.psum_pool(name="psum", bufs=1))
+
+        def held(shape, dtype, name):
+            return keep.tile(shape, dtype, name=name, align_bytes=64)
+
+        offsets = keep.tile([P, S // LIST_ROWS], U16, name="offsets")
+        offsets2 = keep.tile([P, M // LIST_ROWS], U16, name="offsets2")
+        w2w_raw = held([P, H_PASSES * N // 2], I32, "w2w_raw")
+        w2s_raw = held([P, H_PASSES * N // 4], I32, "w2s_raw")
+        tabs_raw = held([P, T // 4], I32, "tabs_raw")
+        tabw_raw = [held([P, T], I32, "tabw_raw%d" % a) for a in range(K_PASSES)]
+
+        nc.vector.memset(tabs_raw[:], 0)
+        nc.vector.memset(w2s_raw[:], 0)
+
+        def load_table(a):
+            nc.sync.dma_start(
+                out=tabw_raw[a][:],
+                in_=tab_words[a].rearrange("p t i -> p (t i)").bitcast(I32))
+
+        def load_rows(rows, name, own=False):
+            if own:
+                raw = keep.tile([P, PACK, BANK], F32, name=name, tag="looked0", align_bytes=64)
+            else:
+                raw = raws.tile([P, PACK, BANK], F32, name=name, tag="raw")
+            nc.sync.dma_start(out=raw[:], in_=rows.rearrange("(p j) c -> p j c", j=PACK))
+            return raw
+
+        def load_w1(a, b):
+            return load_rows(w1[a * PASS:(a + 1) * PASS, b * PASS:(b + 1) * PASS], "w1raw%d%d" % (a, b), (a, b) == (0, 1))
+
+        def load_vec(vec, name):
+            t = keep.tile([P, H_PASSES, PACK], F32, name=name, tag=name, align_bytes=64)
+            nc.sync.dma_start(out=t[:], in_=vec.rearrange("(b p i) -> p b i", b=H_PASSES, i=PACK))
+            return t
+
+        load_table(0)
+        nc.sync.dma_start(offsets[:], offs)
+        w1raw = {}
+        w1raw[0, 0] = load_w1(0, 0)
+        for q in range(4):
+            live = slice(32 * q, 32 * q + 4 * K_PASSES)
+            nc.sync.dma_start(out=tabs_raw[live, :], in_=tab_scales.bitcast(I32)[:, 4 * q:4 * q + 4, :])
+        w1raw[1, 0] = load_w1(1, 0)
+        load_table(1)
+        w1raw[2, 0] = load_w1(2, 0)
+        level_t = load_vec(level, "level_t")
+        steep_t = load_vec(steep, "steep_t")
+        share_t = load_vec(share, "share_t")
+        load_table(2)
+        nc.sync.dma_start(offsets2[:], offs2)
+
+        vw = [[held([P, BANK], U32, "vw%d%d" % (a, s)) for s in range(2)] for a in range(K_PASSES)]
+        vs = [held([P, BANK], U8, "vs%d" % s) for s in range(2)]
+        cols = BANK // LIST_ROWS
+
+        def gather_words(a):
+            for s in range(2):
+                nc.vector.tensor_copy(
+                    out=vw[a][s][:],
+                    in_=tabw_raw[a][:].bitcast(U32).indirect(offsets[:, s * cols:(s + 1) * cols]))
+
+        def gather_scales():
+            for s in range(2):
+                nc.vector.tensor_copy(
+                    out=vs[s][:],
+                    in_=tabs_raw[:].bitcast(U8).indirect(offsets[:, s * cols:(s + 1) * cols]))
+
+        def weave_weight(copy, raw, t0, nt, name):
+            g = woven.tile([P, PACK * BANK], BF16, name=name, tag="woven", align_bytes=64)
+            part = g[:, :nt * BANK]
+            copy(out=part.rearrange("p (t m j) -> p m j t", t=nt, j=PACK),
+                 in_=raw[:].rearrange("p j (m t) -> p m j t", t=PACK)[:, :, :, t0:t0 + nt])
+            return part
+
+        def quantise(part, name):
+            width = part.shape[1] // PACK
+            codes = held([P, width], U32, name + "_c")
+            scales = held([P, width], U8, name + "_s")
+            nc.vector.quantize_mx(out=codes[:].bitcast(FP8X4), scales=scales[:], in_=part)
+            return codes, scales
+
+        w1q = {}
+
+        def note_slices(table, key, t0, nt, made):
+            codes, scales = made
+            for t in range(nt):
+                table[key + (t0 + t,)] = (codes[:, t * P:(t + 1) * P], scales[:, t * P:(t + 1) * P])
+
+        banks = {}
+
+        def first_product(a, b, i):
+            codes, scales = w1q[a, b, i]
+            for s in range(2):
+                if a == 0:
+                    banks[b, i, s] = psum.tile([P, BANK], F32, name="h%d%d%d" % (b, i, s), tag="bank%d" % (2 * i + s))
+                nc.tensor.matmul_mx(
+                    out=banks[b, i, s][:], lhsT=codes.bitcast(FP8X4), lhsT_scale=scales,
+                    rhs=vw[a][s][:].bitcast(FP8X4), rhs_scale=vs[s][4 * a:, :],
+                    start=(a == 0), stop=(a == K_PASSES - 1))
+
+        gather_words(0)
+        gather_scales()
+        for a in range(2):
+            part = weave_weight(nc.scalar.copy, w1raw[a, 0], 0, PACK, "w1g%d0" % a)
+            note_slices(w1q, (a, 0), 0, PACK, quantise(part, "w1q%d0" % a))
+            if a > 0:
+                gather_words(a)
+            for i in range(PACK):
+                first_product(a, 0, i)
+        early = weave_weight(nc.vector.tensor_copy, w1raw[2, 0], 0, 2, "w1g20a")
+        late = weave_weight(nc.scalar.copy, w1raw[2, 0], 2, 2, "w1g20b")
+        note_slices(w1q, (2, 0), 0, 2, quantise(early, "w1q20a"))
+        note_slices(w1q, (2, 0), 2, 2, quantise(late, "w1q20b"))
+        gather_words(2)
+        for i in range(PACK):
+            first_product(2, 0, i)
+
+        for a in range(K_PASSES):
+            w1raw[a, 1] = load_w1(a, 1)
+        gain_t = load_vec(gain, "gain_t")
+        pat = [held([P, PACK, M], F32, "pat0")]
+        w3raw = []
+        nc.sync.dma_start(out=pat[0][:], in_=pattern[:PASS, :].rearrange("(p j) c -> p j c", j=PACK))
+        for b in range(H_PASSES):
+            w3raw.append(load_rows(w3[b * PASS:(b + 1) * PASS, :], "w3raw%d" % b))
+        nc.sync.dma_start(
+            out=w2w_raw[:].rearrange("p (a c) -> p a c", a=H_PASSES),
+            in_=w2_words.bitcast(I32).rearrange("a p c -> p a c"))
+        for q in range(4):
+            nc.sync.dma_start(
+                out=w2s_raw[32 * q:32 * q + 4, :].rearrange("r (a c) -> r a c", a=H_PASSES),
+                in_=w2_scales.bitcast(I32)[:, 4 * q:4 * q + 4, :].rearrange("a r c -> r a c"))
+        pat.append(load_rows(pattern[PASS:, :], "pat1"))
+
+        slope = keep.tile([P, H_PASSES, PACK], F32, name="slope", tag="slope", align_bytes=64)
+        nc.vector.scalar_tensor_tensor(
+            out=slope[:], in0=steep_t[:], scalar=-1.0, in1=share_t[:], op0=ALU.mult, op1=ALU.mult)
+
+        h = {}
+        bias = {}
+
+        def empty_h(b, i):
+            ht = hpool.tile([P, S], F32, name="h%d%d" % (b, i), tag="h")
+            tops = held([P, 3], F32, "tops%d%d" % (b, i))
+            for s in range(2):
+                nc.vector.tensor_scalar(
+                    out=ht[:, s * BANK:(s + 1) * BANK], in0=banks[b, i, s][:],
+                    scalar1=level_t[:, b, i:i + 1], scalar2=None, op0=ALU.add, op1=ALU.max,
+                    accum_out=tops[:, s:s + 1])
+            nc.vector.tensor_scalar(
+                out=tops[:, 2:3], in0=tops[:, 0:1], scalar1=tops[:, 1:2], scalar2=slope[:, b, i:i + 1],
+                op0=ALU.max, op1=ALU.mult)
+            h[b, i] = ht
+            bias[b, i] = tops[:, 2:3]
+
+        def look_plain(b, i, dst, lst):
+            nc.scalar.activation(out=dst[:, i, :], in_=h[b, i][:].indirect(lst), func=ACT.Copy)
+
+        def look_gate(b, i, dst, lst):
+            nc.scalar.activation(
+                out=dst[:, i, :], in_=h[b, i][:].indirect(lst), func=ACT.Sigmoid,
+                bias=bias[b, i], scale=steep_t[:, b, i:i + 1])
+
+        def weave_product(picked, factor, name, after=None):
+            width = picked.shape[2]
+            if after is None:
+                g = woven.tile([P, PACK * BANK], BF16, name=name, tag="woven", align_bytes=64)
+            else:
+                g = keep.tile([P, PACK * BANK], BF16, name=name, tag=after, align_bytes=64)
+            part = g[:, :PACK * width]
+            nc.vector.tensor_tensor(
+                out=part.rearrange("p (c e i) -> p c i e", e=4, i=PACK),
+                in0=picked[:, :, :].rearrange("p i (c e) -> p c i e", e=4),
+                in1=factor, op=ALU.mult)
+            return part
+
+        def gain_view(b, width):
+            return gain_t[:, b, :].unsqueeze(1).unsqueeze(3).to_broadcast([P, width // 4, PACK, 4])
+
+        def pattern_view(b, m0, width):
+            return pat[b][:, :, m0:m0 + width].rearrange("p i (c e) -> p c i e", e=4)
+
+        ahead = weave_weight(nc.scalar.copy, w1raw[0, 1], 0, PACK, "w1g01")
+        looked0 = keep.tile([P, 2 * PACK, M], F32, name="looked0", tag="looked0", align_bytes=64)
+        plain0 = looked0[:, :PACK, :]
+        gate0 = looked0[:, PACK:, :]
+        for i in range(PACK):
+            empty_h(0, i)
+            look_plain(0, i, plain0, offsets2[:])
+            look_gate(0, i, gate0, offsets2[:])
+            if i < K_PASSES:
+                a = i
+                part = ahead if a == 0 else weave_weight(nc.vector.tensor_copy, w1raw[a, 1], 0, PACK, "w1g%d1" % a)
+                note_slices(w1q, (a, 1), 0, PACK, quantise(part, "w1q%d1" % a))
+        for a in range(K_PASSES):
+            for i in range(PACK):
+                first_product(a, 1, i)
+
+        w3g = [weave_weight(nc.scalar.copy, w3raw[b], 0, PACK, "w3g%d" % b) for b in range(H_PASSES)]
+
+        lists = [offsets2[:, u * HALF // LIST_ROWS:(u + 1) * HALF // LIST_ROWS] for u in range(2)]
+        gate1 = [held([P, PACK, HALF], F32, "gate1%d" % u) for u in range(2)]
+        plain1 = [held([P, PACK, HALF], F32, "plain1%d" % u) for u in range(2)]
+        for i in range(PACK):
+            empty_h(1, i)
+            look_plain(1, i, plain1[0], lists[0])
+            look_gate(1, i, gate1[0], lists[0])
+        for i in range(PACK):
+            look_plain(1, i, plain1[1], lists[1])
+        for i in range(PACK):
+            look_gate(1, i, gate1[1], lists[1])
+
+        w3q = {}
+        z0g = weave_product(plain0, gain_view(0, M), "z0g", after="level_t")
+        x0g = weave_product(gate0, pattern_view(0, 0, M), "x0g", after="slope")
+        z0 = quantise(z0g, "z0")
+        x0 = quantise(x0g, "x0")
+        for b in range(H_PASSES):
+            note_slices(w3q, (b,), 0, PACK, quantise(w3g[b], "w3q%d" % b))
+
+        w2w = held([P, H_PASSES, 2 * N], U8, "w2w")
+        w2s = held([P, H_PASSES, N], U8, "w2s")
+        nc.vector.tensor_copy(
+            out=w2w[:].rearrange("p a c -> p (a c)").bitcast(U16).rearrange("p (a t m) -> p a m t", a=H_PASSES, t=PACK),
+            in_=w2w_raw[:].bitcast(U16).rearrange("p (a m t) -> p a m t", a=H_PASSES, t=PACK))
+        nc.vector.tensor_copy(
+            out=w2s[:].rearrange("p a (t m) -> p a m t", t=PACK),
+            in_=w2s_raw[:].bitcast(U8).rearrange("p (a m t) -> p a m t", a=H_PASSES, t=PACK))
+
+        ybank = {}
+
+        def second_product(u, t, lhs, lhs_scale, moving, m0, first, last):
+            codes, scales = moving
+            nc.tensor.matmul_mx(
+                out=ybank[u, t // 2][:, (t % 2) * HALF:(t % 2 + 1) * HALF],
+                lhsT=lhs, lhsT_scale=lhs_scale,
+                rhs=codes[:, m0:m0 + HALF].bitcast(FP8X4), rhs_scale=scales[:, m0:m0 + HALF],
+                start=first, stop=last)
+
+        def with_w3(u, b, moving, m0, first):
+            for t in range(PACK):
+                codes, scales = w3q[b, t]
+                second_product(u, t, codes.bitcast(FP8X4), scales, moving, m0, first and t % 2 == 0, False)
+
+        def with_w2(u, b, moving, m0, last):
+            for t in range(PACK):
+                second_product(
+                    u, t, w2w[:, b, 2 * P * t:2 * P * (t + 1)].bitcast(FP4X4), w2s[:, b, P * t:P * (t + 1)],
+                    moving, m0, False, last and t % 2 == 1)
+
+        for u in range(2):
+            for v in range(2):
+                ybank[u, v] = psum.tile([P, BANK], F32, name="y%d%d" % (u, v), tag="bank%d" % (2 * u + v))
+            with_w3(u, 0, z0, u * HALF, True)
+            with_w2(u, 0, x0, u * HALF, False)
+
+        out_rows = out_0.rearrange("(p t) m -> p t m", t=PACK)
+        out_words = out_1[0].rearrange("p m t -> p (m t)").bitcast(I32)
+        out_scales = out_2[0].bitcast(I32)
+        for u in range(2):
+            zg = weave_product(plain1[u], gain_view(1, HALF), "z1g%d" % u)
+            xg = weave_product(gate1[u], pattern_view(1, u * HALF, HALF), "x1g%d" % u)
+            z1 = quantise(zg, "z1%d" % u)
+            x1 = quantise(xg, "x1%d" % u)
+            with_w3(u, 1, z1, 0, False)
+            with_w2(u, 1, x1, 0, True)
+
+        for u in range(2):
+            y = held([P, PACK, HALF], F32, "y%d" % u)
+            flat = y[:].rearrange("p t m -> p (t m)")
+            (nc.scalar.copy if u == 0 else nc.vector.tensor_copy)(out=flat[:, :BANK], in_=ybank[u, 0][:])
+            nc.scalar.copy(out=flat[:, BANK:], in_=ybank[u, 1][:])
+            nc.sync.dma_start(out=out_rows[:, :, u * HALF:(u + 1) * HALF], in_=y[:])
+            yg = held([P, PACK * HALF], BF16, "yg%d" % u)
+            nc.vector.tensor_copy(
+                out=yg[:].rearrange("p (c e t) -> p c t e", e=4, t=PACK),
+                in_=y[:].rearrange("p t (c e) -> p c t e", e=4))
+            codes, scales = quantise(yg[:], "yq%d" % u)
+            nc.scalar.dma_start(out=out_words[:, u * HALF:(u + 1) * HALF], in_=codes[:].bitcast(I32))
+            for q in range(4):
+                queue = nc.sync if q % 2 == 0 else nc.scalar
+                queue.dma_start(
+                    out=out_scales[4 * q:4 * q + 4, u * HALF // 4:(u + 1) * HALF // 4],
+                    in_=scales[32 * q:32 * q + 4, :].bitcast(I32))

@@ -34,8 +34,7 @@ def tile_list_flank_contact_features_kernel(
     with ExitStack() as ctx:
         keep = ctx.enter_context(tc.tile_pool(name="keep", bufs=1))
         raws = ctx.enter_context(tc.tile_pool(name="raws", bufs=5))
-        woven = ctx.enter_context(tc.tile_pool(name="woven", bufs=3))
-        hpool = ctx.enter_context(tc.tile_pool(name="hpool", bufs=6))
+        woven = ctx.enter_context(tc.tile_pool(name="woven", bufs=4))
         psum = ctx.enter_context(tc.psum_pool(name="psum", bufs=1))
 
         def held(shape, dtype, name):
@@ -56,16 +55,16 @@ def tile_list_flank_contact_features_kernel(
                 out=tabw_raw[a][:],
                 in_=tab_words[a].rearrange("p t i -> p (t i)").bitcast(I32))
 
-        def load_rows(rows, name, own=False):
+        def load_rows(rows, name, own=None):
             if own:
-                raw = keep.tile([P, PACK, BANK], F32, name=name, tag="looked0", align_bytes=64)
+                raw = keep.tile([P, PACK, BANK], F32, name=name, tag=own, align_bytes=64)
             else:
                 raw = raws.tile([P, PACK, BANK], F32, name=name, tag="raw")
             nc.sync.dma_start(out=raw[:], in_=rows.rearrange("(p j) c -> p j c", j=PACK))
             return raw
 
         def load_w1(a, b):
-            return load_rows(w1[a * PASS:(a + 1) * PASS, b * PASS:(b + 1) * PASS], "w1raw%d%d" % (a, b), (a, b) == (0, 1))
+            return load_rows(w1[a * PASS:(a + 1) * PASS, b * PASS:(b + 1) * PASS], "w1raw%d%d" % (a, b), {(0, 1): "plain0"}.get((a, b)))
 
         def load_vec(vec, name):
             t = keep.tile([P, H_PASSES, PACK], F32, name=name, tag=name, align_bytes=64)
@@ -80,6 +79,13 @@ def tile_list_flank_contact_features_kernel(
             live = slice(32 * q, 32 * q + 4 * K_PASSES)
             nc.sync.dma_start(out=tabs_raw[live, :], in_=tab_scales.bitcast(I32)[:, 4 * q:4 * q + 4, :])
         w1raw[1, 0] = load_w1(1, 0)
+        nc.sync.dma_start(
+            out=w2w_raw[:].rearrange("p (a c) -> p a c", a=H_PASSES),
+            in_=w2_words.bitcast(I32).rearrange("a p c -> p a c"))
+        for q in range(4):
+            nc.sync.dma_start(
+                out=w2s_raw[32 * q:32 * q + 4, :].rearrange("r (a c) -> r a c", a=H_PASSES),
+                in_=w2_scales.bitcast(I32)[:, 4 * q:4 * q + 4, :].rearrange("a r c -> r a c"))
         load_table(1)
         w1raw[2, 0] = load_w1(2, 0)
         level_t = load_vec(level, "level_t")
@@ -104,21 +110,45 @@ def tile_list_flank_contact_features_kernel(
                     out=vs[s][:],
                     in_=tabs_raw[:].bitcast(U8).indirect(offsets[:, s * cols:(s + 1) * cols]))
 
-        def weave_weight(copy, raw, t0, nt, name):
-            g = woven.tile([P, PACK * BANK], BF16, name=name, tag="woven", align_bytes=64)
+        def weave_weight(copy, raw, t0, nt, name, own=None):
+            if own:
+                g = keep.tile([P, PACK * BANK], BF16, name=name, tag=own, align_bytes=64)
+            else:
+                g = woven.tile([P, PACK * BANK], BF16, name=name, tag="woven", align_bytes=64)
             part = g[:, :nt * BANK]
             copy(out=part.rearrange("p (t m j) -> p m j t", t=nt, j=PACK),
                  in_=raw[:].rearrange("p j (m t) -> p m j t", t=PACK)[:, :, :, t0:t0 + nt])
             return part
 
-        def quantise(part, name):
+        def weave_on_gpsimd(raw, part):
+            for half in range(2):
+                m = slice(half * P // 2, (half + 1) * P // 2)
+                nc.gpsimd.tensor_scalar(
+                    out=part.rearrange("p (t m j) -> p m t j", t=PACK, j=PACK)[:, m],
+                    in0=raw[:].rearrange("p j (m t) -> p m t j", t=PACK)[:, m],
+                    scalar1=1.0, scalar2=0.0, op0=ALU.mult, op1=ALU.add)
+            return part
+
+        def quantise(part, name, after=None):
             width = part.shape[1] // PACK
-            codes = held([P, width], U32, name + "_c")
+            codes = keep.tile([P, width], U32, name=name + "_c", tag=after or name + "_c", align_bytes=64)
             scales = held([P, width], U8, name + "_s")
             nc.vector.quantize_mx(out=codes[:].bitcast(FP8X4), scales=scales[:], in_=part)
             return codes, scales
 
         w1q = {}
+
+        w2w = held([P, H_PASSES, 2 * N], U8, "w2w")
+        w2s = held([P, H_PASSES, N], U8, "w2s")
+
+        def deal_w2():
+            nc.vector.tensor_copy(
+                out=w2w[:].rearrange("p a c -> p (a c)").bitcast(U16).rearrange("p (a t m) -> p a m t", a=H_PASSES, t=PACK),
+                in_=w2w_raw[:].bitcast(U16).rearrange("p (a m t) -> p a m t", a=H_PASSES, t=PACK))
+            nc.vector.tensor_copy(
+                out=w2s[:].rearrange("p a (t m) -> p a m t", t=PACK),
+                in_=w2s_raw[:].bitcast(U8).rearrange("p (a m t) -> p a m t", a=H_PASSES, t=PACK))
+
 
         def note_slices(table, key, t0, nt, made):
             codes, scales = made
@@ -144,6 +174,8 @@ def tile_list_flank_contact_features_kernel(
             note_slices(w1q, (a, 0), 0, PACK, quantise(part, "w1q%d0" % a))
             if a > 0:
                 gather_words(a)
+            else:
+                deal_w2()
             for i in range(PACK):
                 first_product(a, 0, i)
         early = weave_weight(nc.vector.tensor_copy, w1raw[2, 0], 0, 2, "w1g20a")
@@ -162,13 +194,6 @@ def tile_list_flank_contact_features_kernel(
         nc.sync.dma_start(out=pat[0][:], in_=pattern[:PASS, :].rearrange("(p j) c -> p j c", j=PACK))
         for b in range(H_PASSES):
             w3raw.append(load_rows(w3[b * PASS:(b + 1) * PASS, :], "w3raw%d" % b))
-        nc.sync.dma_start(
-            out=w2w_raw[:].rearrange("p (a c) -> p a c", a=H_PASSES),
-            in_=w2_words.bitcast(I32).rearrange("a p c -> p a c"))
-        for q in range(4):
-            nc.sync.dma_start(
-                out=w2s_raw[32 * q:32 * q + 4, :].rearrange("r (a c) -> r a c", a=H_PASSES),
-                in_=w2_scales.bitcast(I32)[:, 4 * q:4 * q + 4, :].rearrange("a r c -> r a c"))
         pat.append(load_rows(pattern[PASS:, :], "pat1"))
 
         slope = keep.tile([P, H_PASSES, PACK], F32, name="slope", tag="slope", align_bytes=64)
@@ -179,18 +204,18 @@ def tile_list_flank_contact_features_kernel(
         bias = {}
 
         def empty_h(b, i):
-            ht = hpool.tile([P, S], F32, name="h%d%d" % (b, i), tag="h")
-            tops = held([P, 3], F32, "tops%d%d" % (b, i))
+            ht = held([P, S], F32, "h%d%d" % (b, i))
+            tops = held([P, 16], F32, "tops%d%d" % (b, i))
             for s in range(2):
                 nc.vector.tensor_scalar(
                     out=ht[:, s * BANK:(s + 1) * BANK], in0=banks[b, i, s][:],
                     scalar1=level_t[:, b, i:i + 1], scalar2=None, op0=ALU.add, op1=ALU.max,
                     accum_out=tops[:, s:s + 1])
             nc.vector.tensor_scalar(
-                out=tops[:, 2:3], in0=tops[:, 0:1], scalar1=tops[:, 1:2], scalar2=slope[:, b, i:i + 1],
+                out=tops[:, 8:9], in0=tops[:, 0:1], scalar1=tops[:, 1:2], scalar2=slope[:, b, i:i + 1],
                 op0=ALU.max, op1=ALU.mult)
             h[b, i] = ht
-            bias[b, i] = tops[:, 2:3]
+            bias[b, i] = tops[:, 8:9]
 
         def look_plain(b, i, dst, lst):
             nc.scalar.activation(out=dst[:, i, :], in_=h[b, i][:].indirect(lst), func=ACT.Copy)
@@ -219,23 +244,30 @@ def tile_list_flank_contact_features_kernel(
         def pattern_view(b, m0, width):
             return pat[b][:, :, m0:m0 + width].rearrange("p i (c e) -> p c i e", e=4)
 
-        ahead = weave_weight(nc.scalar.copy, w1raw[0, 1], 0, PACK, "w1g01")
-        looked0 = keep.tile([P, 2 * PACK, M], F32, name="looked0", tag="looked0", align_bytes=64)
-        plain0 = looked0[:, :PACK, :]
-        gate0 = looked0[:, PACK:, :]
+        ahead = [weave_weight(nc.scalar.copy, w1raw[a, 1], 0, PACK, "w1g%d1" % a) for a in range(1)]
+        plain0 = keep.tile([P, PACK, M], F32, name="plain0", tag="plain0", align_bytes=64)
+        gate0 = keep.tile([P, PACK, M], F32, name="gate0", tag="gate0", align_bytes=64)
         for i in range(PACK):
             empty_h(0, i)
             look_plain(0, i, plain0, offsets2[:])
             look_gate(0, i, gate0, offsets2[:])
             if i < K_PASSES:
                 a = i
-                part = ahead if a == 0 else weave_weight(nc.vector.tensor_copy, w1raw[a, 1], 0, PACK, "w1g%d1" % a)
+                if a < 1:
+                    part = ahead[a]
+                else:
+                    last = keep.tile([P, PACK * BANK], BF16, name="w1g%d1" % a, tag=("w1g11", "w3g")[a - 1], align_bytes=64)
+                    part = weave_on_gpsimd(w1raw[a, 1], last[:])
                 note_slices(w1q, (a, 1), 0, PACK, quantise(part, "w1q%d1" % a))
-        for a in range(K_PASSES):
-            for i in range(PACK):
-                first_product(a, 1, i)
+        for wave in range(PACK + K_PASSES - 1):
+            for a in range(K_PASSES):
+                if 0 <= wave - a < PACK:
+                    first_product(a, 1, wave - a)
 
-        w3g = [weave_weight(nc.scalar.copy, w3raw[b], 0, PACK, "w3g%d" % b) for b in range(H_PASSES)]
+        w3both = keep.tile([P, H_PASSES * PACK * BANK], BF16, name="w3both", tag="w3g", align_bytes=64)
+        w3g = [w3both[:, b * PACK * BANK:(b + 1) * PACK * BANK] for b in range(H_PASSES)]
+        for b in range(H_PASSES):
+            weave_on_gpsimd(w3raw[b], w3g[b])
 
         lists = [offsets2[:, u * HALF // LIST_ROWS:(u + 1) * HALF // LIST_ROWS] for u in range(2)]
         gate1 = [held([P, PACK, HALF], F32, "gate1%d" % u) for u in range(2)]
@@ -255,16 +287,7 @@ def tile_list_flank_contact_features_kernel(
         z0 = quantise(z0g, "z0")
         x0 = quantise(x0g, "x0")
         for b in range(H_PASSES):
-            note_slices(w3q, (b,), 0, PACK, quantise(w3g[b], "w3q%d" % b))
-
-        w2w = held([P, H_PASSES, 2 * N], U8, "w2w")
-        w2s = held([P, H_PASSES, N], U8, "w2s")
-        nc.vector.tensor_copy(
-            out=w2w[:].rearrange("p a c -> p (a c)").bitcast(U16).rearrange("p (a t m) -> p a m t", a=H_PASSES, t=PACK),
-            in_=w2w_raw[:].bitcast(U16).rearrange("p (a m t) -> p a m t", a=H_PASSES, t=PACK))
-        nc.vector.tensor_copy(
-            out=w2s[:].rearrange("p a (t m) -> p a m t", t=PACK),
-            in_=w2s_raw[:].bitcast(U8).rearrange("p (a m t) -> p a m t", a=H_PASSES, t=PACK))
+            note_slices(w3q, (b,), 0, PACK, quantise(w3g[b], "w3q%d" % b, ("level_t", "slope")[b]))
 
         ybank = {}
 
@@ -297,7 +320,18 @@ def tile_list_flank_contact_features_kernel(
         out_words = out_1[0].rearrange("p m t -> p (m t)").bitcast(I32)
         out_scales = out_2[0].bitcast(I32)
         for u in range(2):
-            zg = weave_product(plain1[u], gain_view(1, HALF), "z1g%d" % u)
+            if u == 0:
+                planes = held([P, PACK, HALF], BF16, "z1planes")
+                for i in range(PACK):
+                    nc.scalar.activation(
+                        out=planes[:, i, :], in_=plain1[u][:, i, :], func=ACT.Copy, scale=gain_t[:, 1, i:i + 1])
+                zt = woven.tile([P, PACK * BANK], BF16, name="z1g0", tag="woven", align_bytes=64)
+                zg = zt[:, :PACK * HALF]
+                nc.scalar.copy(
+                    out=zg.rearrange("p (c e i) -> p c i e", e=4, i=PACK),
+                    in_=planes[:].rearrange("p i (c e) -> p c i e", e=4))
+            else:
+                zg = weave_product(plain1[u], gain_view(1, HALF), "z1g%d" % u)
             xg = weave_product(gate1[u], pattern_view(1, u * HALF, HALF), "x1g%d" % u)
             z1 = quantise(zg, "z1%d" % u)
             x1 = quantise(xg, "x1%d" % u)
@@ -311,7 +345,7 @@ def tile_list_flank_contact_features_kernel(
             nc.scalar.copy(out=flat[:, BANK:], in_=ybank[u, 1][:])
             nc.sync.dma_start(out=out_rows[:, :, u * HALF:(u + 1) * HALF], in_=y[:])
             yg = held([P, PACK * HALF], BF16, "yg%d" % u)
-            nc.vector.tensor_copy(
+            (nc.scalar.copy if u == 0 else nc.vector.tensor_copy)(
                 out=yg[:].rearrange("p (c e t) -> p c t e", e=4, t=PACK),
                 in_=y[:].rearrange("p t (c e) -> p c t e", e=4))
             codes, scales = quantise(yg[:], "yq%d" % u)

@@ -64,7 +64,7 @@ def tile_list_flank_contact_features_kernel(
             return raw
 
         def load_w1(a, b):
-            return load_rows(w1[a * PASS:(a + 1) * PASS, b * PASS:(b + 1) * PASS], "w1raw%d%d" % (a, b), {(0, 1): "plain0"}.get((a, b)))
+            return load_rows(w1[a * PASS:(a + 1) * PASS, b * PASS:(b + 1) * PASS], "w1raw%d%d" % (a, b), {(0, 1): "looked0"}.get((a, b)))
 
         def load_vec(vec, name):
             t = keep.tile([P, H_PASSES, PACK], F32, name=name, tag=name, align_bytes=64)
@@ -203,19 +203,22 @@ def tile_list_flank_contact_features_kernel(
         h = {}
         bias = {}
 
-        def empty_h(b, i):
-            ht = held([P, S], F32, "h%d%d" % (b, i))
-            tops = held([P, 16], F32, "tops%d%d" % (b, i))
-            for s in range(2):
-                nc.vector.tensor_scalar(
-                    out=ht[:, s * BANK:(s + 1) * BANK], in0=banks[b, i, s][:],
-                    scalar1=level_t[:, b, i:i + 1], scalar2=None, op0=ALU.add, op1=ALU.max,
-                    accum_out=tops[:, s:s + 1])
+        tops = {}
+
+        def empty_bank(b, i, s):
+            if s == 0:
+                h[b, i] = keep.tile([P, S], F32, name="h%d%d" % (b, i), tag="h%d%d" % (b, i), align_bytes=64)
+                tops[b, i] = held([P, 3], F32, "tops%d%d" % (b, i))
             nc.vector.tensor_scalar(
-                out=tops[:, 8:9], in0=tops[:, 0:1], scalar1=tops[:, 1:2], scalar2=slope[:, b, i:i + 1],
+                out=h[b, i][:, s * BANK:(s + 1) * BANK], in0=banks[b, i, s][:],
+                scalar1=level_t[:, b, i:i + 1], scalar2=None, op0=ALU.add, op1=ALU.max,
+                accum_out=tops[b, i][:, s:s + 1])
+
+        def gate_bias(b, i):
+            bias[b, i] = tops[b, i][:, 2:3]
+            nc.vector.tensor_scalar(
+                out=bias[b, i], in0=tops[b, i][:, 0:1], scalar1=tops[b, i][:, 1:2], scalar2=slope[:, b, i:i + 1],
                 op0=ALU.max, op1=ALU.mult)
-            h[b, i] = ht
-            bias[b, i] = tops[:, 8:9]
 
         def look_plain(b, i, dst, lst):
             nc.scalar.activation(out=dst[:, i, :], in_=h[b, i][:].indirect(lst), func=ACT.Copy)
@@ -244,25 +247,26 @@ def tile_list_flank_contact_features_kernel(
         def pattern_view(b, m0, width):
             return pat[b][:, :, m0:m0 + width].rearrange("p i (c e) -> p c i e", e=4)
 
-        ahead = [weave_weight(nc.scalar.copy, w1raw[a, 1], 0, PACK, "w1g%d1" % a) for a in range(1)]
-        plain0 = keep.tile([P, PACK, M], F32, name="plain0", tag="plain0", align_bytes=64)
-        gate0 = keep.tile([P, PACK, M], F32, name="gate0", tag="gate0", align_bytes=64)
+        ahead = [weave_weight(nc.scalar.copy, w1raw[a, 1], 0, PACK, "w1g%d1" % a, "h01") for a in range(1)]
+        looked0 = keep.tile([P, 2 * PACK, M], F32, name="looked0", tag="looked0", align_bytes=64)
+        plain0 = looked0[:, :PACK, :]
+        gate0 = looked0[:, PACK:, :]
         for i in range(PACK):
-            empty_h(0, i)
-            look_plain(0, i, plain0, offsets2[:])
-            look_gate(0, i, gate0, offsets2[:])
+            empty_bank(0, i, 0)
+            empty_bank(0, i, 1)
             if i < K_PASSES:
                 a = i
                 if a < 1:
                     part = ahead[a]
                 else:
-                    last = keep.tile([P, PACK * BANK], BF16, name="w1g%d1" % a, tag=("w1g11", "w3g")[a - 1], align_bytes=64)
+                    last = keep.tile([P, PACK * BANK], BF16, name="w1g%d1" % a, tag="h0%d" % (a + 1), align_bytes=64)
                     part = weave_on_gpsimd(w1raw[a, 1], last[:])
                 note_slices(w1q, (a, 1), 0, PACK, quantise(part, "w1q%d1" % a))
-        for wave in range(PACK + K_PASSES - 1):
-            for a in range(K_PASSES):
-                if 0 <= wave - a < PACK:
-                    first_product(a, 1, wave - a)
+            gate_bias(0, i)
+            look_plain(0, i, plain0, offsets2[:])
+            look_gate(0, i, gate0, offsets2[:])
+        for ready, i, a in sorted((max(2 * i, 2 * a + 1), i, a) for i in range(PACK) for a in range(K_PASSES)):
+            first_product(a, 1, i)
 
         w3both = keep.tile([P, H_PASSES * PACK * BANK], BF16, name="w3both", tag="w3g", align_bytes=64)
         w3g = [w3both[:, b * PACK * BANK:(b + 1) * PACK * BANK] for b in range(H_PASSES)]
@@ -272,8 +276,12 @@ def tile_list_flank_contact_features_kernel(
         lists = [offsets2[:, u * HALF // LIST_ROWS:(u + 1) * HALF // LIST_ROWS] for u in range(2)]
         gate1 = [held([P, PACK, HALF], F32, "gate1%d" % u) for u in range(2)]
         plain1 = [held([P, PACK, HALF], F32, "plain1%d" % u) for u in range(2)]
+        empty_bank(1, 0, 0)
         for i in range(PACK):
-            empty_h(1, i)
+            empty_bank(1, i, 1)
+            if i + 1 < PACK:
+                empty_bank(1, i + 1, 0)
+            gate_bias(1, i)
             look_plain(1, i, plain1[0], lists[0])
             look_gate(1, i, gate1[0], lists[0])
         for i in range(PACK):
@@ -320,7 +328,7 @@ def tile_list_flank_contact_features_kernel(
         out_words = out_1[0].rearrange("p m t -> p (m t)").bitcast(I32)
         out_scales = out_2[0].bitcast(I32)
         for u in range(2):
-            if u == 0:
+            if u == 1:
                 planes = held([P, PACK, HALF], BF16, "z1planes")
                 for i in range(PACK):
                     nc.scalar.activation(

@@ -88,10 +88,10 @@ def tile_list_flank_contact_features_kernel(
                 in_=w2_scales.bitcast(I32)[:, 4 * q:4 * q + 4, :].rearrange("a r c -> r a c"))
         load_table(1)
         w1raw[2, 0] = load_w1(2, 0)
+        load_table(2)
         level_t = load_vec(level, "level_t")
         steep_t = load_vec(steep, "steep_t")
         share_t = load_vec(share, "share_t")
-        load_table(2)
         nc.sync.dma_start(offsets2[:], offs2)
 
         vw = [[held([P, BANK], U32, "vw%d%d" % (a, s)) for s in range(2)] for a in range(K_PASSES)]
@@ -259,8 +259,11 @@ def tile_list_flank_contact_features_kernel(
                 if a < 1:
                     part = ahead[a]
                 else:
-                    last = keep.tile([P, PACK * BANK], BF16, name="w1g%d1" % a, tag="h0%d" % (a + 1), align_bytes=64)
-                    part = weave_on_gpsimd(w1raw[a, 1], last[:])
+                    if a == 1:
+                        last = keep.tile([P, PACK * BANK], BF16, name="w1g11", tag="h02", align_bytes=64)
+                        part = weave_on_gpsimd(w1raw[a, 1], last[:])
+                    else:
+                        part = weave_weight(nc.vector.tensor_copy, w1raw[a, 1], 0, PACK, "w1g21", "w3g")
                 note_slices(w1q, (a, 1), 0, PACK, quantise(part, "w1q%d1" % a))
             gate_bias(0, i)
             look_plain(0, i, plain0, offsets2[:])

@@ -116,8 +116,8 @@ def tile_list_flank_contact_features_kernel(
             else:
                 g = woven.tile([P, PACK * BANK], BF16, name=name, tag="woven", align_bytes=64)
             part = g[:, :nt * BANK]
-            copy(out=part.rearrange("p (t m j) -> p m j t", t=nt, j=PACK),
-                 in_=raw[:].rearrange("p j (m t) -> p m j t", t=PACK)[:, :, :, t0:t0 + nt])
+            copy(out=part.rearrange("p (r t m j) -> p r m j t", t=2, m=P, j=PACK),
+                 in_=raw[:].rearrange("p j (m r t) -> p r m j t", t=2, m=P)[:, t0 // 2:(t0 + nt) // 2])
             return part
 
         def weave_on_gpsimd(raw, part):
@@ -236,16 +236,16 @@ def tile_list_flank_contact_features_kernel(
                 g = keep.tile([P, PACK * BANK], BF16, name=name, tag=after, align_bytes=64)
             part = g[:, :PACK * width]
             nc.vector.tensor_tensor(
-                out=part.rearrange("p (c e i) -> p c i e", e=4, i=PACK),
-                in0=picked[:, :, :].rearrange("p i (c e) -> p c i e", e=4),
+                out=part.rearrange("p (c e i) -> p c i e", e=2, i=PACK),
+                in0=picked[:, :, :].rearrange("p i (c e) -> p c i e", e=2),
                 in1=factor, op=ALU.mult)
             return part
 
         def gain_view(b, width):
-            return gain_t[:, b, :].unsqueeze(1).unsqueeze(3).to_broadcast([P, width // 4, PACK, 4])
+            return gain_t[:, b, :].unsqueeze(1).unsqueeze(3).to_broadcast([P, width // 2, PACK, 2])
 
         def pattern_view(b, m0, width):
-            return pat[b][:, :, m0:m0 + width].rearrange("p i (c e) -> p c i e", e=4)
+            return pat[b][:, :, m0:m0 + width].rearrange("p i (c e) -> p c i e", e=2)
 
         ahead = [weave_weight(nc.scalar.copy, w1raw[a, 1], 0, PACK, "w1g%d1" % a, "h01") for a in range(1)]
         looked0 = keep.tile([P, 2 * PACK, M], F32, name="looked0", tag="looked0", align_bytes=64)
@@ -339,8 +339,8 @@ def tile_list_flank_contact_features_kernel(
                 zt = woven.tile([P, PACK * BANK], BF16, name="z1g0", tag="woven", align_bytes=64)
                 zg = zt[:, :PACK * HALF]
                 nc.scalar.copy(
-                    out=zg.rearrange("p (c e i) -> p c i e", e=4, i=PACK),
-                    in_=planes[:].rearrange("p i (c e) -> p c i e", e=4))
+                    out=zg.rearrange("p (c e i) -> p c i e", e=2, i=PACK),
+                    in_=planes[:].rearrange("p i (c e) -> p c i e", e=2))
             else:
                 zg = weave_product(plain1[u], gain_view(1, HALF), "z1g%d" % u)
             xg = weave_product(gate1[u], pattern_view(1, u * HALF, HALF), "x1g%d" % u)
@@ -357,8 +357,8 @@ def tile_list_flank_contact_features_kernel(
             nc.sync.dma_start(out=out_rows[:, :, u * HALF:(u + 1) * HALF], in_=y[:])
             yg = held([P, PACK * HALF], BF16, "yg%d" % u)
             (nc.scalar.copy if u == 0 else nc.vector.tensor_copy)(
-                out=yg[:].rearrange("p (c e t) -> p c t e", e=4, t=PACK),
-                in_=y[:].rearrange("p t (c e) -> p c t e", e=4))
+                out=yg[:].rearrange("p (c e t) -> p c t e", e=2, t=PACK),
+                in_=y[:].rearrange("p t (c e) -> p c t e", e=2))
             codes, scales = quantise(yg[:], "yq%d" % u)
             nc.scalar.dma_start(out=out_words[:, u * HALF:(u + 1) * HALF], in_=codes[:].bitcast(I32))
             for q in range(4):

from contextlib import ExitStack

import concourse.mybir as mybir

K, H, N, T, S, M = 1536, 1024, 512, 2048, 1024, 512
FLOPS = 2 * K * H * S + 2 * 2 * H * N * M

F32 = mybir.dt.float32
BF16 = mybir.dt.bfloat16
I32 = mybir.dt.int32
U32 = mybir.dt.uint32
U16 = mybir.dt.uint16
U8 = mybir.dt.uint8
FP8X4 = mybir.dt.float8_e4m3fn_x4
FP4X4 = mybir.dt.float4_e2m1fn_x4
ALU = mybir.AluOpType
ACT = mybir.ActivationFunctionType

P = 128
PACK = 4
PASS = P * PACK
K_PASSES = K // PASS
H_PASSES = H // PASS
BANK = 512
HALF = M // 2
LIST_ROWS = 16


def tile_list_flank_contact_features_kernel(
    tc, tab_words, tab_scales, offs, offs2, w1, level, steep, share, pattern, gain,
    w2_words, w2_scales, w3, out_0, out_1, out_2,
):
    nc = tc.nc
    with ExitStack() as ctx:
        keep = ctx.enter_context(tc.tile_pool(name="keep", bufs=1))
        raws = ctx.enter_context(tc.tile_pool(name="raws", bufs=5))
        woven = ctx.enter_context(tc.tile_pool(name="woven", bufs=4))
        psum = ctx.enter_context(tc.psum_pool(name="psum", bufs=1))

        def held(shape, dtype, name):
            return keep.tile(shape, dtype, name=name, align_bytes=64)

        offsets = keep.tile([P, S // LIST_ROWS], U16, name="offsets")
        offsets2 = keep.tile([P, M // LIST_ROWS], U16, name="offsets2")
        w2w_raw = held([P, H_PASSES * N // 2], I32, "w2w_raw")
        w2s_raw = held([P, H_PASSES * N // 4], I32, "w2s_raw")
        tabs_raw = held([P, T // 4], I32, "tabs_raw")
        tabw_raw = [held([P, T], I32, "tabw_raw%d" % a) for a in range(K_PASSES)]

        nc.vector.memset(tabs_raw[:], 0)
        nc.vector.memset(w2s_raw[:], 0)

        def load_table(a):
            nc.sync.dma_start(
                out=tabw_raw[a][:],
                in_=tab_words[a].rearrange("p t i -> p (t i)").bitcast(I32))

        def load_rows(rows, name, own=None):
            if own:
                raw = keep.tile([P, PACK, BANK], F32, name=name, tag=own, align_bytes=64)
            else:
                raw = raws.tile([P, PACK, BANK], F32, name=name, tag="raw")
            nc.sync.dma_start(out=raw[:], in_=rows.rearrange("(p j) c -> p j c", j=PACK))
            return raw

        def load_w1(a, b):
            return load_rows(w1[a * PASS:(a + 1) * PASS, b * PASS:(b + 1) * PASS], "w1raw%d%d" % (a, b), {(0, 1): "looked0"}.get((a, b)))

        def load_vec(vec, name):
            t = keep.tile([P, H_PASSES, PACK], F32, name=name, tag=name, align_bytes=64)
            nc.sync.dma_start(out=t[:], in_=vec.rearrange("(b p i) -> p b i", b=H_PASSES, i=PACK))
            return t

        load_table(0)
        nc.sync.dma_start(offsets[:], offs)
        w1raw = {}
        w1raw[0, 0] = load_w1(0, 0)
        for q in range(4):
            live = slice(32 * q, 32 * q + 4 * K_PASSES)
            nc.sync.dma_start(out=tabs_raw[live, :], in_=tab_scales.bitcast(I32)[:, 4 * q:4 * q + 4, :])
        w1raw[1, 0] = load_w1(1, 0)
        nc.sync.dma_start(
            out=w2w_raw[:].rearrange("p (a c) -> p a c", a=H_PASSES),
            in_=w2_words.bitcast(I32).rearrange("a p c -> p a c"))
        for q in range(4):
            nc.sync.dma_start(
                out=w2s_raw[32 * q:32 * q + 4, :].rearrange("r (a c) -> r a c", a=H_PASSES),
                in_=w2_scales.bitcast(I32)[:, 4 * q:4 * q + 4, :].rearrange("a r c -> r a c"))
        load_table(1)
        w1raw[2, 0] = load_w1(2, 0)
        load_table(2)
        level_t = load_vec(level, "level_t")
        steep_t = load_vec(steep, "steep_t")
        share_t = load_vec(share, "share_t")
        nc.sync.dma_start(offsets2[:], offs2)

        vw = [[held([P, BANK], U32, "vw%d%d" % (a, s)) for s in range(2)] for a in range(K_PASSES)]
        vs = [held([P, BANK], U8, "vs%d" % s) for s in range(2)]
        cols = BANK // LIST_ROWS

        def gather_words(a):
            for s in range(2):
                nc.vector.tensor_copy(
                    out=vw[a][s][:],
                    in_=tabw_raw[a][:].bitcast(U32).indirect(offsets[:, s * cols:(s + 1) * cols]))

        def gather_scales():
            for s in range(2):
                nc.vector.tensor_copy(
                    out=vs[s][:],
                    in_=tabs_raw[:].bitcast(U8).indirect(offsets[:, s * cols:(s + 1) * cols]))

        def weave_weight(copy, raw, t0, nt, name, own=None):
            if own:
                g = keep.tile([P, PACK * BANK], BF16, name=name, tag=own, align_bytes=64)
            else:
                g = woven.tile([P, PACK * BANK], BF16, name=name, tag="woven", align_bytes=64)
            part = g[:, :nt * BANK]
            copy(out=part.rearrange("p (r t m j) -> p r m j t", t=2, m=P, j=PACK),
                 in_=raw[:].rearrange("p j (m r t) -> p r m j t", t=2, m=P)[:, t0 // 2:(t0 + nt) // 2])
            return part

        def weave_on_gpsimd(raw, part):
            for half in range(2):
                m = slice(half * P // 2, (half + 1) * P // 2)
                nc.gpsimd.tensor_scalar(
                    out=part.rearrange("p (t m j) -> p m t j", t=PACK, j=PACK)[:, m],
                    in0=raw[:].rearrange("p j (m t) -> p m t j", t=PACK)[:, m],
                    scalar1=1.0, scalar2=0.0, op0=ALU.mult, op1=ALU.add)
            return part

        def quantise(part, name, after=None):
            width = part.shape[1] // PACK
            codes = keep.tile([P, width], U32, name=name + "_c", tag=after or name + "_c", align_bytes=64)
            scales = held([P, width], U8, name + "_s")
            nc.vector.quantize_mx(out=codes[:].bitcast(FP8X4), scales=scales[:], in_=part)
            return codes, scales

        w1q = {}

        w2w = held([P, H_PASSES, 2 * N], U8, "w2w")
        w2s = held([P, H_PASSES, N], U8, "w2s")

        def deal_w2():
            nc.vector.tensor_copy(
                out=w2w[:].rearrange("p a c -> p (a c)").bitcast(U16).rearrange("p (a t m) -> p a m t", a=H_PASSES, t=PACK),
                in_=w2w_raw[:].bitcast(U16).rearrange("p (a m t) -> p a m t", a=H_PASSES, t=PACK))
            nc.vector.tensor_copy(
                out=w2s[:].rearrange("p a (t m) -> p a m t", t=PACK),
                in_=w2s_raw[:].bitcast(U8).rearrange("p (a m t) -> p a m t", a=H_PASSES, t=PACK))


        def note_slices(table, key, t0, nt, made):
            codes, scales = made
            for t in range(nt):
                table[key + (t0 + t,)] = (codes[:, t * P:(t + 1) * P], scales[:, t * P:(t + 1) * P])

        banks = {}

        def first_product(a, b, i):
            codes, scales = w1q[a, b, i]
            for s in range(2):
                if a == 0:
                    banks[b, i, s] = psum.tile([P, BANK], F32, name="h%d%d%d" % (b, i, s), tag="bank%d" % (2 * i + s))
                nc.tensor.matmul_mx(
                    out=banks[b, i, s][:], lhsT=codes.bitcast(FP8X4), lhsT_scale=scales,
                    rhs=vw[a][s][:].bitcast(FP8X4), rhs_scale=vs[s][4 * a:, :],
                    start=(a == 0), stop=(a == K_PASSES - 1))

        gather_words(0)
        gather_scales()
        for a in range(2):
            part = weave_weight(nc.scalar.copy, w1raw[a, 0], 0, PACK, "w1g%d0" % a)
            note_slices(w1q, (a, 0), 0, PACK, quantise(part, "w1q%d0" % a))
            if a > 0:
                gather_words(a)
            else:
                deal_w2()
            for i in range(PACK):
                first_product(a, 0, i)
        early = weave_weight(nc.vector.tensor_copy, w1raw[2, 0], 0, 2, "w1g20a")
        late = weave_weight(nc.scalar.copy, w1raw[2, 0], 2, 2, "w1g20b")
        note_slices(w1q, (2, 0), 0, 2, quantise(early, "w1q20a"))
        note_slices(w1q, (2, 0), 2, 2, quantise(late, "w1q20b"))
        gather_words(2)
        for i in range(PACK):
            first_product(2, 0, i)

        for a in range(K_PASSES):
            w1raw[a, 1] = load_w1(a, 1)
        gain_t = load_vec(gain, "gain_t")
        pat = [held([P, PACK, M], F32, "pat0")]
        w3raw = []
        nc.sync.dma_start(out=pat[0][:], in_=pattern[:PASS, :].rearrange("(p j) c -> p j c", j=PACK))
        for b in range(H_PASSES):
            w3raw.append(load_rows(w3[b * PASS:(b + 1) * PASS, :], "w3raw%d" % b))
        pat.append(load_rows(pattern[PASS:, :], "pat1"))

        slope = keep.tile([P, H_PASSES, PACK], F32, name="slope", tag="slope", align_bytes=64)
        nc.vector.scalar_tensor_tensor(
            out=slope[:], in0=steep_t[:], scalar=-1.0, in1=share_t[:], op0=ALU.mult, op1=ALU.mult)

        h = {}
        bias = {}

        tops = {}

        def empty_bank(b, i, s):
            if s == 0:
                h[b, i] = keep.tile([P, S], F32, name="h%d%d" % (b, i), tag="h%d%d" % (b, i), align_bytes=64)
                tops[b, i] = held([P, 3], F32, "tops%d%d" % (b, i))
            nc.vector.tensor_scalar(
                out=h[b, i][:, s * BANK:(s + 1) * BANK], in0=banks[b, i, s][:],
                scalar1=level_t[:, b, i:i + 1], scalar2=None, op0=ALU.add, op1=ALU.max,
                accum_out=tops[b, i][:, s:s + 1])

        def gate_bias(b, i):
            bias[b, i] = tops[b, i][:, 2:3]
            nc.vector.tensor_scalar(
                out=bias[b, i], in0=tops[b, i][:, 0:1], scalar1=tops[b, i][:, 1:2], scalar2=slope[:, b, i:i + 1],
                op0=ALU.max, op1=ALU.mult)

        def look_plain(b, i, dst, lst):
            nc.scalar.activation(out=dst[:, i, :], in_=h[b, i][:].indirect(lst), func=ACT.Copy)

        def look_gate(b, i, dst, lst):
            nc.scalar.activation(
                out=dst[:, i, :], in_=h[b, i][:].indirect(lst), func=ACT.Sigmoid,
                bias=bias[b, i], scale=steep_t[:, b, i:i + 1])

        def weave_product(picked, factor, name, after=None):
            width = picked.shape[2]
            if after is None:
                g = woven.tile([P, PACK * BANK], BF16, name=name, tag="woven", align_bytes=64)
            else:
                g = keep.tile([P, PACK * BANK], BF16, name=name, tag=after, align_bytes=64)
            part = g[:, :PACK * width]
            nc.vector.tensor_tensor(
                out=part.rearrange("p (c e i) -> p c i e", e=2, i=PACK),
                in0=picked[:, :, :].rearrange("p i (c e) -> p c i e", e=2),
                in1=factor, op=ALU.mult)
            return part

        def gain_view(b, width):
            return gain_t[:, b, :].unsqueeze(1).unsqueeze(3).to_broadcast([P, width // 2, PACK, 2])

        def pattern_view(b, m0, width):
            return pat[b][:, :, m0:m0 + width].rearrange("p i (c e) -> p c i e", e=2)

        ahead = [weave_weight(nc.scalar.copy, w1raw[a, 1], 0, PACK, "w1g%d1" % a, "h01") for a in range(1)]
        looked0 = keep.tile([P, 2 * PACK, M], F32, name="looked0", tag="looked0", align_bytes=64)
        plain0 = looked0[:, :PACK, :]
        gate0 = looked0[:, PACK:, :]
        for i in range(PACK):
            empty_bank(0, i, 0)
            empty_bank(0, i, 1)
            if i < K_PASSES:
                a = i
                if a < 1:
                    part = ahead[a]
                else:
                    if a == 1:
                        last = keep.tile([P, PACK * BANK], BF16, name="w1g11", tag="h02", align_bytes=64)
                        part = weave_on_gpsimd(w1raw[a, 1], last[:])
                    else:
                        part = weave_weight(nc.vector.tensor_copy, w1raw[a, 1], 0, PACK, "w1g21", "w3g")
                note_slices(w1q, (a, 1), 0, PACK, quantise(part, "w1q%d1" % a))
            gate_bias(0, i)
            look_plain(0, i, plain0, offsets2[:])
            look_gate(0, i, gate0, offsets2[:])
        for ready, i, a in sorted((max(2 * i, 2 * a + 1), i, a) for i in range(PACK) for a in range(K_PASSES)):
            first_product(a, 1, i)

        w3both = keep.tile([P, H_PASSES * PACK * BANK], BF16, name="w3both", tag="w3g", align_bytes=64)
        w3g = [w3both[:, b * PACK * BANK:(b + 1) * PACK * BANK] for b in range(H_PASSES)]
        for b in range(H_PASSES):
            weave_on_gpsimd(w3raw[b], w3g[b])

        lists = [offsets2[:, u * HALF // LIST_ROWS:(u + 1) * HALF // LIST_ROWS] for u in range(2)]
        gate1 = [held([P, PACK, HALF], F32, "gate1%d" % u) for u in range(2)]
        plain1 = [held([P, PACK, HALF], F32, "plain1%d" % u) for u in range(2)]
        empty_bank(1, 0, 0)
        for i in range(PACK):
            empty_bank(1, i, 1)
            if i + 1 < PACK:
                empty_bank(1, i + 1, 0)
            gate_bias(1, i)
            look_plain(1, i, plain1[0], lists[0])
            look_gate(1, i, gate1[0], lists[0])
        for i in range(PACK):
            look_plain(1, i, plain1[1], lists[1])
        for i in range(PACK):
            look_gate(1, i, gate1[1], lists[1])

        w3q = {}
        z0g = weave_product(plain0, gain_view(0, M), "z0g", after="level_t")
        x0g = weave_product(gate0, pattern_view(0, 0, M), "x0g", after="slope")
        z0 = quantise(z0g, "z0")
        x0 = quantise(x0g, "x0")
        for b in range(H_PASSES):
            note_slices(w3q, (b,), 0, PACK, quantise(w3g[b], "w3q%d" % b, ("level_t", "slope")[b]))

        ybank = {}

        def second_product(u, t, lhs, lhs_scale, moving, m0, first, last):
            codes, scales = moving
            nc.tensor.matmul_mx(
                out=ybank[u, t // 2][:, (t % 2) * HALF:(t % 2 + 1) * HALF],
                lhsT=lhs, lhsT_scale=lhs_scale,
                rhs=codes[:, m0:m0 + HALF].bitcast(FP8X4), rhs_scale=scales[:, m0:m0 + HALF],
                start=first, stop=last)

        def with_w3(u, b, moving, m0, first):
            for t in range(PACK):
                codes, scales = w3q[b, t]
                second_product(u, t, codes.bitcast(FP8X4), scales, moving, m0, first and t % 2 == 0, False)

        def with_w2(u, b, moving, m0, last):
            for t in range(PACK):
                second_product(
                    u, t, w2w[:, b, 2 * P * t:2 * P * (t + 1)].bitcast(FP4X4), w2s[:, b, P * t:P * (t + 1)],
                    moving, m0, False, last and t % 2 == 1)

        for u in range(2):
            for v in range(2):
                ybank[u, v] = psum.tile([P, BANK], F32, name="y%d%d" % (u, v), tag="bank%d" % (2 * u + v))
            with_w3(u, 0, z0, u * HALF, True)
            with_w2(u, 0, x0, u * HALF, False)

        out_rows = out_0.rearrange("(p t) m -> p t m", t=PACK)
        out_words = out_1[0].rearrange("p m t -> p (m t)").bitcast(I32)
        out_scales = out_2[0].bitcast(I32)
        for u in range(2):
            if u == 1:
                planes = held([P, PACK, HALF], BF16, "z1planes")
                for i in range(PACK):
                    nc.scalar.activation(
                        out=planes[:, i, :], in_=plain1[u][:, i, :], func=ACT.Copy, scale=gain_t[:, 1, i:i + 1])
                zt = woven.tile([P, PACK * BANK], BF16, name="z1g0", tag="woven", align_bytes=64)
                zg = zt[:, :PACK * HALF]
                nc.scalar.copy(
                    out=zg.rearrange("p (c e i) -> p c i e", e=2, i=PACK),
                    in_=planes[:].rearrange("p i (c e) -> p c i e", e=2))
            else:
                zg = weave_product(plain1[u], gain_view(1, HALF), "z1g%d" % u)
            xg = weave_product(gate1[u], pattern_view(1, u * HALF, HALF), "x1g%d" % u)
            z1 = quantise(zg, "z1%d" % u)
            x1 = quantise(xg, "x1%d" % u)
            with_w3(u, 1, z1, 0, False)
            with_w2(u, 1, x1, 0, True)

        for u in range(2):
            y = held([P, PACK, HALF], F32, "y%d" % u)
            flat = y[:].rearrange("p t m -> p (t m)")
            (nc.scalar.copy if u == 0 else nc.vector.tensor_copy)(out=flat[:, :BANK], in_=ybank[u, 0][:])
            nc.scalar.copy(out=flat[:, BANK:], in_=ybank[u, 1][:])
            nc.sync.dma_start(out=out_rows[:, :, u * HALF:(u + 1) * HALF], in_=y[:])
            yg = held([P, PACK * HALF], BF16, "yg%d" % u)
            (nc.scalar.copy if u == 0 else nc.vector.tensor_copy)(
                out=yg[:].rearrange("p (c e t) -> p c t e", e=2, t=PACK),
                in_=y[:].rearrange("p t (c e) -> p c t e", e=2))
            codes, scales = quantise(yg[:], "yq%d" % u)
            nc.scalar.dma_start(out=out_words[:, u * HALF:(u + 1) * HALF], in_=codes[:].bitcast(I32))
            for q in range(4):
                queue = nc.sync if q % 2 == 0 else nc.scalar
                queue.dma_start(
                    out=out_scales[4 * q:4 * q + 4, u * HALF // 4:(u + 1) * HALF // 4],
                    in_=scales[32 * q:32 * q + 4, :].bitcast(I32))
